import numpy as np
import ml_dtypes


def mxq(x, axis, fmt="e4m3"):
    dtype, down = {"e4m3": (ml_dtypes.float8_e4m3fn, 7), "e5m2": (ml_dtypes.float8_e5m2, 14)}[fmt]
    v = np.moveaxis(np.asarray(x, np.float32).astype(ml_dtypes.bfloat16).astype(np.float64), axis, -1)
    blocks = v.reshape(v.shape[:-1] + (-1, 32))
    amax = np.abs(blocks).max(-1, keepdims=True)
    byte = np.maximum(np.where(amax > 0, np.frexp(amax)[1] - 1 + 127, 0) - down, 1)
    scale = np.exp2(byte - 127.0)
    codes = (blocks / scale).astype(np.float32).astype(dtype).astype(np.float64)
    return np.moveaxis((codes * scale).reshape(v.shape), -1, axis)


WIDE = False


def mx_kscale(k):
    if not WIDE:
        return np.ones(k)
    levels = np.array([10, -10, 5, -5, 0])
    if k % 512:
        return np.exp2(np.random.permutation(np.resize(levels, k // 32))).repeat(32)
    a = np.empty((k // 512, 16))
    for p in range(k // 512):
        a[p, :8] = np.random.permutation(np.resize(levels, 8))
        for g in range(8):
            far = levels[np.abs(levels - a[p, g]) >= 10]
            a[p, g + 8] = far[np.random.randint(len(far))]
    return np.exp2(a.ravel()).repeat(32)


def f64(x):
    return np.asarray(x).astype(np.float64)


def striped(idx):
    return np.tile(np.asarray(idx).reshape(-1, 16).T, (8, 1)).astype(np.uint16)


def unstriped(offs):
    return offs[:16].T.reshape(-1).astype(np.int64)


E2M1 = np.array([0.0, 0.5, 1.0, 1.5, 2.0, 3.0, 4.0, 6.0, -0.0, -0.5, -1.0, -1.5, -2.0, -3.0, -4.0, -6.0])


def pack_weight(w, fmt):
    k, n = w.shape
    w = f64(np.asarray(w, np.float32).astype(ml_dtypes.bfloat16)).reshape(k // 32, 32, n)
    amax = np.abs(w).max(1)
    if fmt == "e4m3":
        byte = np.frexp(amax)[1] - 1 + 127 - 7
    else:
        mant, ex = np.frexp(amax / 6.0)
        byte = np.where(mant > 0.5, ex, ex - 1) + 127
    byte = np.clip(np.where(amax > 0, byte, 1), 1, 254)
    scaled = (w * np.exp2(127.0 - byte)[:, None, :]).reshape(k, n).astype(np.float32)
    by_word = np.ascontiguousarray(scaled.reshape(k // 512, 128, 4, n).transpose(0, 1, 3, 2))
    if fmt == "e4m3":
        words = by_word.astype(ml_dtypes.float8_e4m3fn).view(np.uint8)
    else:
        c = by_word.astype(ml_dtypes.float4_e2m1fn).view(np.uint8) & 0xF
        words = (c[..., 0::2] | (c[..., 1::2] << 4)).reshape(k // 512, 128, 2 * n)
    return np.ascontiguousarray(words), np.ascontiguousarray(byte.astype(np.uint8).reshape(k // 512, 16, n))


def unpack_weight(words, scales, fmt):
    g, _, n = scales.shape
    words = np.ascontiguousarray(words).reshape(g, 128, n, -1)
    if fmt == "e4m3":
        vals = words.view(ml_dtypes.float8_e4m3fn).astype(np.float64)
    else:
        nib = np.empty((g, 128, n, 4), np.uint8)
        nib[..., 0::2] = words & 0xF
        nib[..., 1::2] = words >> 4
        vals = E2M1[nib]
    vals = vals * np.repeat(np.exp2(scales.astype(np.float64) - 127.0), 8, axis=1)[..., None]
    return vals.transpose(0, 1, 3, 2).reshape(g * 512, n)


K, T, J, R, F, Z, N, S = 512, 1024, 256, 512, 512, 1024, 256, 1024


def setup_inputs():
    n = np.random.standard_normal
    idx = np.random.permutation(T)[:J]
    idx2 = np.random.permutation(Z)[:J]
    idx3 = np.random.permutation(J)[:J]
    idx4 = np.random.permutation(S)[:N]
    fk = mx_kscale(K)
    fr = mx_kscale(R)
    ff = mx_kscale(F)
    wp = pack_weight(n((K, R)) * 1 / np.sqrt(K) / fk[:, None] * fr, "e2m1")
    xop = pack_weight(n((F, Z)) / ff[:, None], "e4m3")
    w2p = pack_weight(n((F, R)) * 1 / np.sqrt(F) * ff[:, None] * fr, "e2m1")
    vsp = pack_weight(n((R, S)) * 1 / np.sqrt(R) / fr[:, None], "e2m1")
    return {
        "cq": (np.random.randint(-7, 8, (K, T)).astype(np.float64)).astype(np.float32),
        "ga": (np.random.uniform(0.1, 0.4, (K, 1)) * fk[:, None]).astype(np.float32),
        "w_words": wp[0],
        "w_scales": wp[1],
        "xo_words": xop[0],
        "xo_scales": xop[1],
        "w2_words": w2p[0],
        "w2_scales": w2p[1],
        "sa": (np.random.uniform(0.5, 1.6, (R, 1))).astype(np.float32),
        "vs_words": vsp[0],
        "vs_scales": vsp[1],
        "offs": striped(idx),
        "offs2": striped(idx2),
        "offs3": striped(idx3),
        "offs4": striped(idx4),
    }


def reference(cq, ga, w_words, w_scales, xo_words, xo_scales, w2_words, w2_scales, sa, vs_words, vs_scales, offs, offs2, offs3, offs4):
    idx = unstriped(offs)
    idx2 = unstriped(offs2)
    idx3 = unstriped(offs3)
    idx4 = unstriped(offs4)
    wu = unpack_weight(w_words, w_scales, "e2m1")
    xou = unpack_weight(xo_words, xo_scales, "e4m3")
    w2u = unpack_weight(w2_words, w2_scales, "e2m1")
    vsu = unpack_weight(vs_words, vs_scales, "e2m1")
    x1 = f64(cq)[:, idx] * f64(ga)
    x1q = mxq(x1, 0, "e4m3")
    xoidx2g = xou[:, idx2]
    a = wu.T @ x1q + w2u.T @ xoidx2g
    hid = np.abs(a - a[:, idx3] * f64(sa))
    vsidx4g = vsu[:, idx4]
    hidq = mxq(hid, 0, "e4m3")
    y = vsidx4g.T @ hidq
    return y

@@ -1,0 +1,183 @@
+from contextlib import ExitStack
+
+import concourse.mybir as mybir
+
+F32 = mybir.dt.float32
+BF16 = mybir.dt.bfloat16
+I32 = mybir.dt.int32
+U32 = mybir.dt.uint32
+U16 = mybir.dt.uint16
+U8 = mybir.dt.uint8
+FP8X4 = mybir.dt.float8_e4m3fn_x4
+FP4X4 = mybir.dt.float4_e2m1fn_x4
+ACT = mybir.ActivationFunctionType
+ALU = mybir.AluOpType
+
+P = 128
+PACK = 4
+TABLE = 1024
+SLOTS = 256
+HIDDEN = 512
+QUAD = 32
+X1_SPLIT = 176
+HID_SPLIT = 144
+
+FLOPS = 2 * 512 * HIDDEN * SLOTS * 2 + 2 * HIDDEN * SLOTS * SLOTS
+
+
+def tile_list_lessneighbour_codedboth_store_plain_kernel(
+    tc, cq, ga, w_words, w_scales, xo_words, xo_scales, w2_words, w2_scales, sa, vs_words, vs_scales,
+    offs, offs2, offs3, offs4, out,
+):
+    nc = tc.nc
+    with ExitStack() as ctx:
+        keep = ctx.enter_context(tc.tile_pool(name="keep", bufs=1))
+        psum = ctx.enter_context(tc.psum_pool(name="psum", bufs=1))
+
+        def tile(name, shape, dtype, tag=None):
+            return keep.tile(shape, dtype, name=name, tag=tag or name, align_bytes=64)
+
+        list1 = tile("list1", [P, SLOTS // 16], U16)
+        list2 = tile("list2", [P, SLOTS // 16], U16)
+        list3 = tile("list3", [P, SLOTS // 16], U16)
+        list4 = tile("list4", [P, SLOTS // 16], U16)
+        ga_sb = tile("ga_sb", [P, PACK], F32)
+        sa_sb = tile("sa_sb", [P, PACK], F32)
+        cq_sb = [tile("cq%d" % t, [P, TABLE], F32) for t in range(PACK)]
+        xo_table = tile("xo_table", [P, TABLE], U32, "xo_then_x1")
+        vs_table = tile("vs_table", [P, TABLE], U16)
+        w_raw = tile("w_raw", [P, HIDDEN], U16)
+        w2_raw = tile("w2_raw", [P, HIDDEN], U16)
+
+        w_stage = tile("w_stage", [P, 4, HIDDEN // 4], I32)
+        w2_stage = tile("w2_stage", [P, 4, HIDDEN // 4], I32)
+        xo_stage = tile("xo_stage", [P, 4, TABLE // 4], I32)
+        vs_stage = tile("vs_stage", [P, 4, TABLE // 4], I32)
+        w_plane = tile("w_plane", [P, HIDDEN], U8)
+        w2_plane = tile("w2_plane", [P, HIDDEN], U8)
+        xo_plane = tile("xo_plane", [P, TABLE], U8)
+        vs_plane = tile("vs_plane", [P, TABLE], U8)
+
+        nc.vector.memset(w2_stage[64:96, :, :], 0)
+        nc.vector.memset(w_plane[:].bitcast(I32), 0)
+        nc.gpsimd.memset(xo_stage[64:96, :, :], 0)
+        nc.vector.memset(vs_plane[:].bitcast(I32), 0)
+
+        def scale_rows(scales):
+            return scales[0].bitcast(I32).rearrange("(q r) n -> r q n", r=4)
+
+        cq_rows = cq.rearrange("(p t) c -> p t c", t=PACK)
+        nc.sync.dma_start(out=cq_sb[0][:], in_=cq_rows[:, 0, :])
+        nc.scalar.dma_start(out=ga_sb[:], in_=ga.rearrange("(p t) o -> p (t o)", t=PACK))
+        nc.sync.dma_start(list1[:], offs)
+        nc.scalar.dma_start(out=w_stage[0:4, :, :], in_=scale_rows(w_scales))
+        nc.sync.dma_start(out=cq_sb[1][:], in_=cq_rows[:, 1, :])
+        nc.scalar.dma_start(out=w2_stage[64:68, :, :], in_=scale_rows(w2_scales))
+        nc.sync.dma_start(list2[:], offs2)
+        nc.sync.dma_start(out=xo_stage[64:68, :, :], in_=scale_rows(xo_scales))
+        nc.sync.dma_start(out=vs_stage[0:4, :, :], in_=scale_rows(vs_scales))
+        nc.sync.dma_start(out=cq_sb[2][:], in_=cq_rows[:, 2, :])
+        nc.sync.dma_start(list4[:], offs4)
+        nc.sync.dma_start(out=cq_sb[3][:], in_=cq_rows[:, 3, :])
+        nc.sync.dma_start(out=xo_table[:].bitcast(I32), in_=xo_words[0].rearrange("p n t -> p (n t)").bitcast(I32))
+        nc.sync.dma_start(out=vs_table[:].bitcast(I32), in_=vs_words[0].bitcast(I32))
+        nc.sync.dma_start(out=w2_raw[:].bitcast(I32), in_=w2_words[0].bitcast(I32))
+        nc.sync.dma_start(out=w_raw[:].bitcast(I32), in_=w_words[0].bitcast(I32))
+        nc.sync.dma_start(list3[:], offs3)
+        nc.sync.dma_start(out=sa_sb[:], in_=sa.rearrange("(p t) o -> p (t o)", t=PACK))
+
+        def spread_low(plane, stage):
+            for q in range(4):
+                nc.vector.tensor_copy(out=plane[QUAD * q : QUAD * q + 4, :].bitcast(I32), in_=stage[0:4, q, :])
+
+        def spread_high(plane, stage):
+            for q in range(4):
+                nc.vector.tensor_copy(out=plane[QUAD * q : QUAD * (q + 1), :].bitcast(I32), in_=stage[64:96, q, :])
+
+        w_scale = tile("w_scale", [P, PACK, P], U8)
+        w2_scale = tile("w2_scale", [P, PACK, P], U8)
+        spread_low(w_plane, w_stage)
+        nc.vector.tensor_copy(out=w_scale[:], in_=w_plane[:].rearrange("p (m t) -> p t m", t=PACK))
+        spread_high(w2_plane, w2_stage)
+        nc.vector.tensor_copy(out=w2_scale[:], in_=w2_plane[:].rearrange("p (m t) -> p t m", t=PACK))
+        spread_high(xo_plane, xo_stage)
+        xo_scale = tile("xo_scale", [P, SLOTS], U8)
+        nc.vector.tensor_copy(xo_scale[:], xo_plane[:].indirect(list2[:]))
+        spread_low(vs_plane, vs_stage)
+        vs_scale = tile("vs_scale", [P, SLOTS], U8)
+        nc.vector.tensor_copy(vs_scale[:], vs_plane[:].indirect(list4[:]))
+
+        x1_rows = tile("x1_rows", [P, PACK, SLOTS], BF16)
+        for t in range(PACK):
+            nc.scalar.activation(out=x1_rows[:, t, :], in_=cq_sb[t][:].indirect(list1[:]), func=ACT.Copy, scale=ga_sb[:, t : t + 1])
+        x1_grouped = tile("x1_grouped", [P, SLOTS, PACK], BF16, "x1_then_vs")
+        nc.vector.tensor_copy(
+            out=x1_grouped[:, :X1_SPLIT, :].rearrange("p (c i) t -> p c t i", i=4),
+            in_=x1_rows[:, :, :X1_SPLIT].rearrange("p t (c i) -> p c t i", i=4),
+        )
+        nc.scalar.copy(
+            out=x1_grouped[:, X1_SPLIT:, :].rearrange("p (c i) t -> p c t i", i=4),
+            in_=x1_rows[:, :, X1_SPLIT:].rearrange("p t (c i) -> p c t i", i=4),
+        )
+        xo_codes = tile("xo_codes", [P, SLOTS], U32)
+        nc.vector.tensor_copy(xo_codes[:], xo_table[:].indirect(list2[:]))
+        x1_codes = tile("x1_codes", [P, SLOTS], U32, "xo_then_x1")
+        x1_scale = tile("x1_scale", [P, SLOTS], U8)
+        nc.vector.quantize_mx(out=x1_codes[:].bitcast(FP8X4), scales=x1_scale[:], in_=x1_grouped[:].rearrange("p c t -> p (c t)"))
+
+        w_codes = tile("w_codes", [P, PACK, P], U16)
+        w2_codes = tile("w2_codes", [P, PACK, P], U16)
+        for t in range(PACK):
+            for raw, codes in ((w2_raw, w2_codes), (w_raw, w_codes)):
+                nc.scalar.copy(out=codes[:, t, :], in_=raw[:].rearrange("p (m t) -> p t m", t=PACK)[:, t, :])
+
+        vs_codes = tile("vs_codes", [P, SLOTS], U16, "x1_then_vs")
+        nc.vector.tensor_copy(vs_codes[:], vs_table[:].indirect(list4[:]))
+        windows = [tile("window%d" % t, [P, 2 * SLOTS], F32) for t in range(PACK)]
+        for t in range(PACK):
+            nc.gpsimd.memset(windows[t][:, SLOTS:], 0.0)
+        partner = tile("partner", [P, PACK, SLOTS], F32)
+        diff = tile("diff", [P, PACK, SLOTS], F32)
+        for t in range(PACK):
+            bank = psum.tile([P, SLOTS], F32, name="hidden", bufs=2)
+            nc.tensor.matmul_mx(
+                out=bank[:], lhsT=w2_codes[:, t, :].bitcast(FP4X4), lhsT_scale=w2_scale[:, t, :],
+                rhs=xo_codes[:].bitcast(FP8X4), rhs_scale=xo_scale[:], start=True, stop=False,
+            )
+            nc.tensor.matmul_mx(
+                out=bank[:], lhsT=w_codes[:, t, :].bitcast(FP4X4), lhsT_scale=w_scale[:, t, :],
+                rhs=x1_codes[:].bitcast(FP8X4), rhs_scale=x1_scale[:], start=False, stop=True,
+            )
+            nc.vector.tensor_copy(out=windows[t][:, :SLOTS], in_=bank[:])
+            nc.scalar.activation(out=partner[:, t, :], in_=windows[t][:].indirect(list3[:]), func=ACT.Copy, scale=sa_sb[:, t : t + 1])
+        for t in range(PACK - 1):
+            nc.vector.tensor_tensor(out=diff[:, t, :], in0=windows[t][:, :SLOTS], in1=partner[:, t, :], op=ALU.subtract)
+        for cols in (slice(0, HID_SPLIT), slice(HID_SPLIT, SLOTS)):
+            nc.vector.tensor_tensor(out=diff[:, PACK - 1, cols], in0=windows[PACK - 1][:, cols], in1=partner[:, PACK - 1, cols], op=ALU.subtract)
+
+        hid_grouped = tile("hid_grouped", [P, SLOTS, PACK], BF16)
+        nc.scalar.activation(
+            out=hid_grouped[:, :HID_SPLIT, :].rearrange("p (c i) t -> p c t i", i=4),
+            in_=diff[:, :, :HID_SPLIT].rearrange("p t (c i) -> p c t i", i=4),
+            func=ACT.Abs,
+        )
+        late = diff[:, :, HID_SPLIT:].rearrange("p t c -> p c t")
+        nc.vector.scalar_tensor_tensor(out=hid_grouped[:, HID_SPLIT:, :], in0=late, scalar=-1.0, in1=late, op0=ALU.mult, op1=ALU.max)
+        hid_codes = tile("hid_codes", [P, SLOTS], U32)
+        hid_scale = tile("hid_scale", [P, SLOTS], U8)
+        nc.vector.quantize_mx(out=hid_codes[:].bitcast(FP8X4), scales=hid_scale[:], in_=hid_grouped[:].rearrange("p c t -> p (c t)"))
+
+        for u in range(2):
+            rows = slice(u * P, (u + 1) * P)
+            acc = psum.tile([P, SLOTS], F32, name="acc%d" % u)
+            nc.tensor.matmul_mx(
+                out=acc[:], lhsT=vs_codes[:, rows].bitcast(FP4X4), lhsT_scale=vs_scale[:, rows],
+                rhs=hid_codes[:].bitcast(FP8X4), rhs_scale=hid_scale[:], start=True, stop=True,
+            )
+            result = tile("result%d" % u, [P, SLOTS], F32)
+            if u == 0:
+                nc.vector.tensor_copy(out=result[:], in_=acc[:])
+                nc.sync.dma_start(out=out[rows, :], in_=result[:])
+            else:
+                nc.scalar.copy(out=result[:], in_=acc[:])
+                nc.scalar.dma_start(out=out[rows, :], in_=result[:])

@@ -20,7 +20,7 @@ SLOTS = 256
 HIDDEN = 512
 QUAD = 32
 X1_SPLIT = 176
-HID_SPLIT = 144
+HALF = 128
 
 FLOPS = 2 * 512 * HIDDEN * SLOTS * 2 + 2 * HIDDEN * SLOTS * SLOTS
 
@@ -32,6 +32,7 @@ def tile_list_lessneighbour_codedboth_store_plain_kernel(
     nc = tc.nc
     with ExitStack() as ctx:
         keep = ctx.enter_context(tc.tile_pool(name="keep", bufs=1))
+        reuse = ctx.enter_context(tc.tile_pool(name="reuse", bufs=1))
         psum = ctx.enter_context(tc.psum_pool(name="psum", bufs=1))
 
         def tile(name, shape, dtype, tag=None):
@@ -49,68 +50,52 @@ def tile_list_lessneighbour_codedboth_store_plain_kernel(
         w_raw = tile("w_raw", [P, HIDDEN], U16)
         w2_raw = tile("w2_raw", [P, HIDDEN], U16)
 
-        w_stage = tile("w_stage", [P, 4, HIDDEN // 4], I32)
-        w2_stage = tile("w2_stage", [P, 4, HIDDEN // 4], I32)
-        xo_stage = tile("xo_stage", [P, 4, TABLE // 4], I32)
-        vs_stage = tile("vs_stage", [P, 4, TABLE // 4], I32)
-        w_plane = tile("w_plane", [P, HIDDEN], U8)
-        w2_plane = tile("w2_plane", [P, HIDDEN], U8)
+        weight_stage = tile("weight_stage", [P, 4, 2, HIDDEN // 4], I32)
+        weight_plane = tile("weight_plane", [P, 2, HIDDEN], U8)
         xo_plane = tile("xo_plane", [P, TABLE], U8)
         vs_plane = tile("vs_plane", [P, TABLE], U8)
 
-        nc.vector.memset(w2_stage[64:96, :, :], 0)
-        nc.vector.memset(w_plane[:].bitcast(I32), 0)
-        nc.gpsimd.memset(xo_stage[64:96, :, :], 0)
+        nc.vector.memset(xo_plane[:].bitcast(I32), 0)
         nc.vector.memset(vs_plane[:].bitcast(I32), 0)
+        nc.vector.memset(weight_plane[:].bitcast(I32), 0)
 
-        def scale_rows(scales):
-            return scales[0].bitcast(I32).rearrange("(q r) n -> r q n", r=4)
+        def load_scale_rows(plane, scales):
+            for q in range(4):
+                nc.sync.dma_start(
+                    out=plane[QUAD * q : QUAD * q + 4, :].bitcast(I32), in_=scales[0].bitcast(I32)[4 * q : 4 * q + 4, :]
+                )
 
+        nc.gpsimd.dma_start(out=ga_sb[:], in_=ga.rearrange("(p t) o -> p (t o)", t=PACK))
+        nc.gpsimd.dma_start(out=sa_sb[:], in_=sa.rearrange("(p t) o -> p (t o)", t=PACK))
+        for i, scales in enumerate((w2_scales, w_scales)):
+            nc.scalar.dma_start(out=weight_stage[0:4, :, i, :], in_=scales[0].bitcast(I32).rearrange("(q r) n -> r q n", r=4))
         cq_rows = cq.rearrange("(p t) c -> p t c", t=PACK)
         nc.sync.dma_start(out=cq_sb[0][:], in_=cq_rows[:, 0, :])
-        nc.scalar.dma_start(out=ga_sb[:], in_=ga.rearrange("(p t) o -> p (t o)", t=PACK))
         nc.sync.dma_start(list1[:], offs)
-        nc.scalar.dma_start(out=w_stage[0:4, :, :], in_=scale_rows(w_scales))
-        nc.sync.dma_start(out=cq_sb[1][:], in_=cq_rows[:, 1, :])
-        nc.scalar.dma_start(out=w2_stage[64:68, :, :], in_=scale_rows(w2_scales))
         nc.sync.dma_start(list2[:], offs2)
-        nc.sync.dma_start(out=xo_stage[64:68, :, :], in_=scale_rows(xo_scales))
-        nc.sync.dma_start(out=vs_stage[0:4, :, :], in_=scale_rows(vs_scales))
-        nc.sync.dma_start(out=cq_sb[2][:], in_=cq_rows[:, 2, :])
+        nc.sync.dma_start(out=cq_sb[1][:], in_=cq_rows[:, 1, :])
         nc.sync.dma_start(list4[:], offs4)
+        nc.sync.dma_start(out=cq_sb[2][:], in_=cq_rows[:, 2, :])
+        load_scale_rows(xo_plane, xo_scales)
         nc.sync.dma_start(out=cq_sb[3][:], in_=cq_rows[:, 3, :])
         nc.sync.dma_start(out=xo_table[:].bitcast(I32), in_=xo_words[0].rearrange("p n t -> p (n t)").bitcast(I32))
+        load_scale_rows(vs_plane, vs_scales)
         nc.sync.dma_start(out=vs_table[:].bitcast(I32), in_=vs_words[0].bitcast(I32))
         nc.sync.dma_start(out=w2_raw[:].bitcast(I32), in_=w2_words[0].bitcast(I32))
         nc.sync.dma_start(out=w_raw[:].bitcast(I32), in_=w_words[0].bitcast(I32))
         nc.sync.dma_start(list3[:], offs3)
-        nc.sync.dma_start(out=sa_sb[:], in_=sa.rearrange("(p t) o -> p (t o)", t=PACK))
 
-        def spread_low(plane, stage):
-            for q in range(4):
-                nc.vector.tensor_copy(out=plane[QUAD * q : QUAD * q + 4, :].bitcast(I32), in_=stage[0:4, q, :])
-
-        def spread_high(plane, stage):
-            for q in range(4):
-                nc.vector.tensor_copy(out=plane[QUAD * q : QUAD * (q + 1), :].bitcast(I32), in_=stage[64:96, q, :])
-
-        w_scale = tile("w_scale", [P, PACK, P], U8)
-        w2_scale = tile("w2_scale", [P, PACK, P], U8)
-        spread_low(w_plane, w_stage)
-        nc.vector.tensor_copy(out=w_scale[:], in_=w_plane[:].rearrange("p (m t) -> p t m", t=PACK))
-        spread_high(w2_plane, w2_stage)
-        nc.vector.tensor_copy(out=w2_scale[:], in_=w2_plane[:].rearrange("p (m t) -> p t m", t=PACK))
-        spread_high(xo_plane, xo_stage)
+        weight_scale = tile("weight_scale", [P, 2, PACK, P], U8)
+        for q in range(4):
+            nc.vector.tensor_copy(out=weight_plane[QUAD * q : QUAD * q + 4, :, :].bitcast(I32), in_=weight_stage[0:4, q, :, :])
+        nc.vector.tensor_copy(out=weight_scale[:], in_=weight_plane[:].rearrange("p w (m t) -> p w t m", t=PACK))
         xo_scale = tile("xo_scale", [P, SLOTS], U8)
         nc.vector.tensor_copy(xo_scale[:], xo_plane[:].indirect(list2[:]))
-        spread_low(vs_plane, vs_stage)
-        vs_scale = tile("vs_scale", [P, SLOTS], U8)
-        nc.vector.tensor_copy(vs_scale[:], vs_plane[:].indirect(list4[:]))
 
         x1_rows = tile("x1_rows", [P, PACK, SLOTS], BF16)
         for t in range(PACK):
             nc.scalar.activation(out=x1_rows[:, t, :], in_=cq_sb[t][:].indirect(list1[:]), func=ACT.Copy, scale=ga_sb[:, t : t + 1])
-        x1_grouped = tile("x1_grouped", [P, SLOTS, PACK], BF16, "x1_then_vs")
+        x1_grouped = reuse.tile([P, SLOTS, PACK], BF16, name="x1_grouped", offset=0, align_bytes=64)
         nc.vector.tensor_copy(
             out=x1_grouped[:, :X1_SPLIT, :].rearrange("p (c i) t -> p c t i", i=4),
             in_=x1_rows[:, :, :X1_SPLIT].rearrange("p t (c i) -> p c t i", i=4),
@@ -131,53 +116,65 @@ def tile_list_lessneighbour_codedboth_store_plain_kernel(
             for raw, codes in ((w2_raw, w2_codes), (w_raw, w_codes)):
                 nc.scalar.copy(out=codes[:, t, :], in_=raw[:].rearrange("p (m t) -> p t m", t=PACK)[:, t, :])
 
-        vs_codes = tile("vs_codes", [P, SLOTS], U16, "x1_then_vs")
+        vs_scale = reuse.tile([P, SLOTS], U8, name="vs_scale", offset=1024, align_bytes=64)
+        nc.vector.tensor_copy(vs_scale[:], vs_plane[:].indirect(list4[:]))
+        vs_codes = reuse.tile([P, SLOTS], U16, name="vs_codes", offset=0, align_bytes=64)
         nc.vector.tensor_copy(vs_codes[:], vs_table[:].indirect(list4[:]))
-        windows = [tile("window%d" % t, [P, 2 * SLOTS], F32) for t in range(PACK)]
-        for t in range(PACK):
-            nc.gpsimd.memset(windows[t][:, SLOTS:], 0.0)
+
+        halves = [slice(h * HALF, (h + 1) * HALF) for h in range(2)]
+        windows = [tile("window%d" % t, [P, SLOTS], F32) for t in range(PACK)]
         partner = tile("partner", [P, PACK, SLOTS], F32)
         diff = tile("diff", [P, PACK, SLOTS], F32)
         for t in range(PACK):
-            bank = psum.tile([P, SLOTS], F32, name="hidden", bufs=2)
-            nc.tensor.matmul_mx(
-                out=bank[:], lhsT=w2_codes[:, t, :].bitcast(FP4X4), lhsT_scale=w2_scale[:, t, :],
-                rhs=xo_codes[:].bitcast(FP8X4), rhs_scale=xo_scale[:], start=True, stop=False,
-            )
-            nc.tensor.matmul_mx(
-                out=bank[:], lhsT=w_codes[:, t, :].bitcast(FP4X4), lhsT_scale=w_scale[:, t, :],
-                rhs=x1_codes[:].bitcast(FP8X4), rhs_scale=x1_scale[:], start=False, stop=True,
-            )
-            nc.vector.tensor_copy(out=windows[t][:, :SLOTS], in_=bank[:])
-            nc.scalar.activation(out=partner[:, t, :], in_=windows[t][:].indirect(list3[:]), func=ACT.Copy, scale=sa_sb[:, t : t + 1])
+            bank = psum.tile([P, SLOTS], F32, name="hidden%d" % t)
+            passes = [
+                (w_codes[:, t, :], weight_scale[:, 1, t, :], x1_codes, x1_scale),
+                (w2_codes[:, t, :], weight_scale[:, 0, t, :], xo_codes, xo_scale),
+            ]
+            if t == 0:
+                passes = passes[::-1]
+            for i, (weights, weight_plane_t, codes, scale) in enumerate(passes):
+                nc.tensor.matmul_mx(
+                    out=bank[:], lhsT=weights.bitcast(FP4X4), lhsT_scale=weight_plane_t,
+                    rhs=codes[:].bitcast(FP8X4), rhs_scale=scale[:], start=(i == 0), stop=(i == 1),
+                )
+            nc.vector.tensor_copy(out=windows[t][:], in_=bank[:])
+            for h in range(2):
+                nc.scalar.activation(
+                    out=partner[:, t, halves[h]], in_=windows[t][:].indirect(list3[:, 8 * h : 8 * h + 8]),
+                    func=ACT.Copy, scale=sa_sb[:, t : t + 1],
+                )
         for t in range(PACK - 1):
-            nc.vector.tensor_tensor(out=diff[:, t, :], in0=windows[t][:, :SLOTS], in1=partner[:, t, :], op=ALU.subtract)
-        for cols in (slice(0, HID_SPLIT), slice(HID_SPLIT, SLOTS)):
+            nc.vector.tensor_tensor(out=diff[:, t, :], in0=windows[t][:], in1=partner[:, t, :], op=ALU.subtract)
+        for cols in halves:
             nc.vector.tensor_tensor(out=diff[:, PACK - 1, cols], in0=windows[PACK - 1][:, cols], in1=partner[:, PACK - 1, cols], op=ALU.subtract)
 
         hid_grouped = tile("hid_grouped", [P, SLOTS, PACK], BF16)
+        early = diff[:, :, halves[0]].rearrange("p t c -> p c t")
+        nc.vector.scalar_tensor_tensor(out=hid_grouped[:, halves[0], :], in0=early, scalar=-1.0, in1=early, op0=ALU.mult, op1=ALU.max)
         nc.scalar.activation(
-            out=hid_grouped[:, :HID_SPLIT, :].rearrange("p (c i) t -> p c t i", i=4),
-            in_=diff[:, :, :HID_SPLIT].rearrange("p t (c i) -> p c t i", i=4),
+            out=hid_grouped[:, halves[1], :].rearrange("p (c i) t -> p c t i", i=4),
+            in_=diff[:, :, halves[1]].rearrange("p t (c i) -> p c t i", i=4),
             func=ACT.Abs,
         )
-        late = diff[:, :, HID_SPLIT:].rearrange("p t c -> p c t")
-        nc.vector.scalar_tensor_tensor(out=hid_grouped[:, HID_SPLIT:, :], in0=late, scalar=-1.0, in1=late, op0=ALU.mult, op1=ALU.max)
         hid_codes = tile("hid_codes", [P, SLOTS], U32)
         hid_scale = tile("hid_scale", [P, SLOTS], U8)
-        nc.vector.quantize_mx(out=hid_codes[:].bitcast(FP8X4), scales=hid_scale[:], in_=hid_grouped[:].rearrange("p c t -> p (c t)"))
-
-        for u in range(2):
-            rows = slice(u * P, (u + 1) * P)
-            acc = psum.tile([P, SLOTS], F32, name="acc%d" % u)
-            nc.tensor.matmul_mx(
-                out=acc[:], lhsT=vs_codes[:, rows].bitcast(FP4X4), lhsT_scale=vs_scale[:, rows],
-                rhs=hid_codes[:].bitcast(FP8X4), rhs_scale=hid_scale[:], start=True, stop=True,
+        results = [tile("result%d" % u, [P, SLOTS], F32) for u in range(2)]
+        for h, cols in enumerate(halves):
+            nc.vector.quantize_mx(
+                out=hid_codes[:, cols].bitcast(FP8X4), scales=hid_scale[:, cols],
+                in_=hid_grouped[:, cols, :].rearrange("p c t -> p (c t)"),
             )
-            result = tile("result%d" % u, [P, SLOTS], F32)
-            if u == 0:
-                nc.vector.tensor_copy(out=result[:], in_=acc[:])
-                nc.sync.dma_start(out=out[rows, :], in_=result[:])
-            else:
-                nc.scalar.copy(out=result[:], in_=acc[:])
-                nc.scalar.dma_start(out=out[rows, :], in_=result[:])
+        for h, cols in enumerate(halves):
+            for u, rows in enumerate(halves):
+                acc = psum.tile([P, HALF], F32, name="acc%d%d" % (h, u))
+                nc.tensor.matmul_mx(
+                    out=acc[:], lhsT=vs_codes[:, rows].bitcast(FP4X4), lhsT_scale=vs_scale[:, rows],
+                    rhs=hid_codes[:, cols].bitcast(FP8X4), rhs_scale=hid_scale[:, cols], start=True, stop=True,
+                )
+                if u == 0:
+                    nc.vector.tensor_copy(out=results[u][:, cols], in_=acc[:])
+                else:
+                    nc.scalar.copy(out=results[u][:, cols], in_=acc[:])
+                queue = nc.scalar if (h, u) == (1, 1) else nc.sync
+                queue.dma_start(out=out[rows, cols], in_=results[u][:, cols])

@@ -19,7 +19,7 @@ TABLE = 1024
 SLOTS = 256
 HIDDEN = 512
 QUAD = 32
-X1_SPLIT = 176
+X1_SPLIT = 48
 HALF = 128
 
 FLOPS = 2 * 512 * HIDDEN * SLOTS * 2 + 2 * HIDDEN * SLOTS * SLOTS
@@ -35,8 +35,8 @@ def tile_list_lessneighbour_codedboth_store_plain_kernel(
         reuse = ctx.enter_context(tc.tile_pool(name="reuse", bufs=1))
         psum = ctx.enter_context(tc.psum_pool(name="psum", bufs=1))
 
-        def tile(name, shape, dtype, tag=None):
-            return keep.tile(shape, dtype, name=name, tag=tag or name, align_bytes=64)
+        def tile(name, shape, dtype):
+            return keep.tile(shape, dtype, name=name, align_bytes=64)
 
         list1 = tile("list1", [P, SLOTS // 16], U16)
         list2 = tile("list2", [P, SLOTS // 16], U16)
@@ -45,8 +45,8 @@ def tile_list_lessneighbour_codedboth_store_plain_kernel(
         ga_sb = tile("ga_sb", [P, PACK], F32)
         sa_sb = tile("sa_sb", [P, PACK], F32)
         cq_sb = [tile("cq%d" % t, [P, TABLE], F32) for t in range(PACK)]
-        xo_table = tile("xo_table", [P, TABLE], U32, "xo_then_x1")
-        vs_table = tile("vs_table", [P, TABLE], U16)
+        xo_table = reuse.tile([P, TABLE], U32, name="xo_table", offset=0, align_bytes=64)
+        vs_table = keep.tile([P, TABLE], U16, name="vs_table", tag="diff", align_bytes=64)
         w_raw = tile("w_raw", [P, HIDDEN], U16)
         w2_raw = tile("w2_raw", [P, HIDDEN], U16)
 
@@ -67,11 +67,11 @@ def tile_list_lessneighbour_codedboth_store_plain_kernel(
 
         nc.gpsimd.dma_start(out=ga_sb[:], in_=ga.rearrange("(p t) o -> p (t o)", t=PACK))
         nc.gpsimd.dma_start(out=sa_sb[:], in_=sa.rearrange("(p t) o -> p (t o)", t=PACK))
-        for i, scales in enumerate((w2_scales, w_scales)):
-            nc.scalar.dma_start(out=weight_stage[0:4, :, i, :], in_=scales[0].bitcast(I32).rearrange("(q r) n -> r q n", r=4))
         cq_rows = cq.rearrange("(p t) c -> p t c", t=PACK)
         nc.sync.dma_start(out=cq_sb[0][:], in_=cq_rows[:, 0, :])
         nc.sync.dma_start(list1[:], offs)
+        for i, scales in enumerate((w2_scales, w_scales)):
+            nc.sync.dma_start(out=weight_stage[0:4, :, i, :], in_=scales[0].bitcast(I32).rearrange("(q r) n -> r q n", r=4))
         nc.sync.dma_start(list2[:], offs2)
         nc.sync.dma_start(out=cq_sb[1][:], in_=cq_rows[:, 1, :])
         nc.sync.dma_start(list4[:], offs4)
@@ -80,9 +80,9 @@ def tile_list_lessneighbour_codedboth_store_plain_kernel(
         nc.sync.dma_start(out=cq_sb[3][:], in_=cq_rows[:, 3, :])
         nc.sync.dma_start(out=xo_table[:].bitcast(I32), in_=xo_words[0].rearrange("p n t -> p (n t)").bitcast(I32))
         load_scale_rows(vs_plane, vs_scales)
-        nc.sync.dma_start(out=vs_table[:].bitcast(I32), in_=vs_words[0].bitcast(I32))
         nc.sync.dma_start(out=w2_raw[:].bitcast(I32), in_=w2_words[0].bitcast(I32))
         nc.sync.dma_start(out=w_raw[:].bitcast(I32), in_=w_words[0].bitcast(I32))
+        nc.sync.dma_start(out=vs_table[:].bitcast(I32), in_=vs_words[0].bitcast(I32))
         nc.sync.dma_start(list3[:], offs3)
 
         weight_scale = tile("weight_scale", [P, 2, PACK, P], U8)
@@ -95,7 +95,7 @@ def tile_list_lessneighbour_codedboth_store_plain_kernel(
         x1_rows = tile("x1_rows", [P, PACK, SLOTS], BF16)
         for t in range(PACK):
             nc.scalar.activation(out=x1_rows[:, t, :], in_=cq_sb[t][:].indirect(list1[:]), func=ACT.Copy, scale=ga_sb[:, t : t + 1])
-        x1_grouped = reuse.tile([P, SLOTS, PACK], BF16, name="x1_grouped", offset=0, align_bytes=64)
+        x1_grouped = tile("x1_grouped", [P, SLOTS, PACK], BF16)
         nc.vector.tensor_copy(
             out=x1_grouped[:, :X1_SPLIT, :].rearrange("p (c i) t -> p c t i", i=4),
             in_=x1_rows[:, :, :X1_SPLIT].rearrange("p t (c i) -> p c t i", i=4),
@@ -106,7 +106,7 @@ def tile_list_lessneighbour_codedboth_store_plain_kernel(
         )
         xo_codes = tile("xo_codes", [P, SLOTS], U32)
         nc.vector.tensor_copy(xo_codes[:], xo_table[:].indirect(list2[:]))
-        x1_codes = tile("x1_codes", [P, SLOTS], U32, "xo_then_x1")
+        x1_codes = reuse.tile([P, SLOTS], U32, name="x1_codes", offset=0, align_bytes=64)
         x1_scale = tile("x1_scale", [P, SLOTS], U8)
         nc.vector.quantize_mx(out=x1_codes[:].bitcast(FP8X4), scales=x1_scale[:], in_=x1_grouped[:].rearrange("p c t -> p (c t)"))
 
@@ -118,7 +118,7 @@ def tile_list_lessneighbour_codedboth_store_plain_kernel(
 
         vs_scale = reuse.tile([P, SLOTS], U8, name="vs_scale", offset=1024, align_bytes=64)
         nc.vector.tensor_copy(vs_scale[:], vs_plane[:].indirect(list4[:]))
-        vs_codes = reuse.tile([P, SLOTS], U16, name="vs_codes", offset=0, align_bytes=64)
+        vs_codes = reuse.tile([P, SLOTS], U16, name="vs_codes", offset=2048, align_bytes=64)
         nc.vector.tensor_copy(vs_codes[:], vs_table[:].indirect(list4[:]))
 
         halves = [slice(h * HALF, (h + 1) * HALF) for h in range(2)]

from contextlib import ExitStack

import concourse.mybir as mybir

F32 = mybir.dt.float32
BF16 = mybir.dt.bfloat16
I32 = mybir.dt.int32
U32 = mybir.dt.uint32
U16 = mybir.dt.uint16
U8 = mybir.dt.uint8
FP8X4 = mybir.dt.float8_e4m3fn_x4
FP4X4 = mybir.dt.float4_e2m1fn_x4
ACT = mybir.ActivationFunctionType
ALU = mybir.AluOpType

P = 128
PACK = 4
TABLE = 1024
SLOTS = 256
HIDDEN = 512
QUAD = 32
X1_SPLIT = 48
HALF = 128

FLOPS = 2 * 512 * HIDDEN * SLOTS * 2 + 2 * HIDDEN * SLOTS * SLOTS


def tile_list_lessneighbour_codedboth_store_plain_kernel(
    tc, cq, ga, w_words, w_scales, xo_words, xo_scales, w2_words, w2_scales, sa, vs_words, vs_scales,
    offs, offs2, offs3, offs4, out,
):
    nc = tc.nc
    with ExitStack() as ctx:
        keep = ctx.enter_context(tc.tile_pool(name="keep", bufs=1))
        reuse = ctx.enter_context(tc.tile_pool(name="reuse", bufs=1))
        psum = ctx.enter_context(tc.psum_pool(name="psum", bufs=1))

        def tile(name, shape, dtype):
            return keep.tile(shape, dtype, name=name, align_bytes=64)

        list1 = tile("list1", [P, SLOTS // 16], U16)
        list2 = tile("list2", [P, SLOTS // 16], U16)
        list3 = tile("list3", [P, SLOTS // 16], U16)
        list4 = tile("list4", [P, SLOTS // 16], U16)
        ga_sb = tile("ga_sb", [P, PACK], F32)
        sa_sb = tile("sa_sb", [P, PACK], F32)
        cq_sb = [tile("cq%d" % t, [P, TABLE], F32) for t in range(PACK)]
        xo_table = reuse.tile([P, TABLE], U32, name="xo_table", offset=0, align_bytes=64)
        vs_table = keep.tile([P, TABLE], U16, name="vs_table", tag="diff", align_bytes=64)
        w_raw = tile("w_raw", [P, HIDDEN], U16)
        w2_raw = tile("w2_raw", [P, HIDDEN], U16)

        weight_stage = tile("weight_stage", [P, 4, 2, HIDDEN // 4], I32)
        weight_plane = tile("weight_plane", [P, 2, HIDDEN], U8)
        xo_plane = tile("xo_plane", [P, TABLE], U8)
        vs_plane = tile("vs_plane", [P, TABLE], U8)

        nc.vector.memset(xo_plane[:].bitcast(I32), 0)
        nc.vector.memset(vs_plane[:].bitcast(I32), 0)
        nc.vector.memset(weight_plane[:].bitcast(I32), 0)

        def load_scale_rows(plane, scales):
            for q in range(4):
                nc.sync.dma_start(
                    out=plane[QUAD * q : QUAD * q + 4, :].bitcast(I32), in_=scales[0].bitcast(I32)[4 * q : 4 * q + 4, :]
                )

        nc.gpsimd.dma_start(out=ga_sb[:], in_=ga.rearrange("(p t) o -> p (t o)", t=PACK))
        nc.gpsimd.dma_start(out=sa_sb[:], in_=sa.rearrange("(p t) o -> p (t o)", t=PACK))
        cq_rows = cq.rearrange("(p t) c -> p t c", t=PACK)
        nc.sync.dma_start(out=cq_sb[0][:], in_=cq_rows[:, 0, :])
        nc.sync.dma_start(list1[:], offs)
        for i, scales in enumerate((w2_scales, w_scales)):
            nc.sync.dma_start(out=weight_stage[0:4, :, i, :], in_=scales[0].bitcast(I32).rearrange("(q r) n -> r q n", r=4))
        nc.sync.dma_start(list2[:], offs2)
        nc.sync.dma_start(out=cq_sb[1][:], in_=cq_rows[:, 1, :])
        nc.sync.dma_start(list4[:], offs4)
        nc.sync.dma_start(out=cq_sb[2][:], in_=cq_rows[:, 2, :])
        load_scale_rows(xo_plane, xo_scales)
        nc.sync.dma_start(out=cq_sb[3][:], in_=cq_rows[:, 3, :])
        nc.sync.dma_start(out=xo_table[:].bitcast(I32), in_=xo_words[0].rearrange("p n t -> p (n t)").bitcast(I32))
        load_scale_rows(vs_plane, vs_scales)
        nc.sync.dma_start(out=w2_raw[:].bitcast(I32), in_=w2_words[0].bitcast(I32))
        nc.sync.dma_start(out=w_raw[:].bitcast(I32), in_=w_words[0].bitcast(I32))
        nc.sync.dma_start(out=vs_table[:].bitcast(I32), in_=vs_words[0].bitcast(I32))
        nc.sync.dma_start(list3[:], offs3)

        weight_scale = tile("weight_scale", [P, 2, PACK, P], U8)
        for q in range(4):
            nc.vector.tensor_copy(out=weight_plane[QUAD * q : QUAD * q + 4, :, :].bitcast(I32), in_=weight_stage[0:4, q, :, :])
        nc.vector.tensor_copy(out=weight_scale[:], in_=weight_plane[:].rearrange("p w (m t) -> p w t m", t=PACK))
        xo_scale = tile("xo_scale", [P, SLOTS], U8)
        nc.vector.tensor_copy(xo_scale[:], xo_plane[:].indirect(list2[:]))

        x1_rows = tile("x1_rows", [P, PACK, SLOTS], BF16)
        for t in range(PACK):
            nc.scalar.activation(out=x1_rows[:, t, :], in_=cq_sb[t][:].indirect(list1[:]), func=ACT.Copy, scale=ga_sb[:, t : t + 1])
        x1_grouped = tile("x1_grouped", [P, SLOTS, PACK], BF16)
        nc.vector.tensor_copy(
            out=x1_grouped[:, :X1_SPLIT, :].rearrange("p (c i) t -> p c t i", i=4),
            in_=x1_rows[:, :, :X1_SPLIT].rearrange("p t (c i) -> p c t i", i=4),
        )
        nc.scalar.copy(
            out=x1_grouped[:, X1_SPLIT:, :].rearrange("p (c i) t -> p c t i", i=4),
            in_=x1_rows[:, :, X1_SPLIT:].rearrange("p t (c i) -> p c t i", i=4),
        )
        xo_codes = tile("xo_codes", [P, SLOTS], U32)
        nc.vector.tensor_copy(xo_codes[:], xo_table[:].indirect(list2[:]))
        x1_codes = reuse.tile([P, SLOTS], U32, name="x1_codes", offset=0, align_bytes=64)
        x1_scale = tile("x1_scale", [P, SLOTS], U8)
        nc.vector.quantize_mx(out=x1_codes[:].bitcast(FP8X4), scales=x1_scale[:], in_=x1_grouped[:].rearrange("p c t -> p (c t)"))

        w_codes = tile("w_codes", [P, PACK, P], U16)
        w2_codes = tile("w2_codes", [P, PACK, P], U16)
        for t in range(PACK):
            for raw, codes in ((w2_raw, w2_codes), (w_raw, w_codes)):
                nc.scalar.copy(out=codes[:, t, :], in_=raw[:].rearrange("p (m t) -> p t m", t=PACK)[:, t, :])

        vs_scale = reuse.tile([P, SLOTS], U8, name="vs_scale", offset=1024, align_bytes=64)
        nc.vector.tensor_copy(vs_scale[:], vs_plane[:].indirect(list4[:]))
        vs_codes = reuse.tile([P, SLOTS], U16, name="vs_codes", offset=2048, align_bytes=64)
        nc.vector.tensor_copy(vs_codes[:], vs_table[:].indirect(list4[:]))

        halves = [slice(h * HALF, (h + 1) * HALF) for h in range(2)]
        windows = [tile("window%d" % t, [P, SLOTS], F32) for t in range(PACK)]
        partner = tile("partner", [P, PACK, SLOTS], F32)
        diff = tile("diff", [P, PACK, SLOTS], F32)
        for t in range(PACK):
            bank = psum.tile([P, SLOTS], F32, name="hidden%d" % t)
            passes = [
                (w_codes[:, t, :], weight_scale[:, 1, t, :], x1_codes, x1_scale),
                (w2_codes[:, t, :], weight_scale[:, 0, t, :], xo_codes, xo_scale),
            ]
            if t == 0:
                passes = passes[::-1]
            for i, (weights, weight_plane_t, codes, scale) in enumerate(passes):
                nc.tensor.matmul_mx(
                    out=bank[:], lhsT=weights.bitcast(FP4X4), lhsT_scale=weight_plane_t,
                    rhs=codes[:].bitcast(FP8X4), rhs_scale=scale[:], start=(i == 0), stop=(i == 1),
                )
            nc.vector.tensor_copy(out=windows[t][:], in_=bank[:])
            for h in range(2):
                nc.scalar.activation(
                    out=partner[:, t, halves[h]], in_=windows[t][:].indirect(list3[:, 8 * h : 8 * h + 8]),
                    func=ACT.Copy, scale=sa_sb[:, t : t + 1],
                )
        for t in range(PACK - 1):
            nc.vector.tensor_tensor(out=diff[:, t, :], in0=windows[t][:], in1=partner[:, t, :], op=ALU.subtract)
        for cols in halves:
            nc.vector.tensor_tensor(out=diff[:, PACK - 1, cols], in0=windows[PACK - 1][:, cols], in1=partner[:, PACK - 1, cols], op=ALU.subtract)

        hid_grouped = tile("hid_grouped", [P, SLOTS, PACK], BF16)
        early = diff[:, :, halves[0]].rearrange("p t c -> p c t")
        nc.vector.scalar_tensor_tensor(out=hid_grouped[:, halves[0], :], in0=early, scalar=-1.0, in1=early, op0=ALU.mult, op1=ALU.max)
        nc.scalar.activation(
            out=hid_grouped[:, halves[1], :].rearrange("p (c i) t -> p c t i", i=4),
            in_=diff[:, :, halves[1]].rearrange("p t (c i) -> p c t i", i=4),
            func=ACT.Abs,
        )
        hid_codes = tile("hid_codes", [P, SLOTS], U32)
        hid_scale = tile("hid_scale", [P, SLOTS], U8)
        results = [tile("result%d" % u, [P, SLOTS], F32) for u in range(2)]
        for h, cols in enumerate(halves):
            nc.vector.quantize_mx(
                out=hid_codes[:, cols].bitcast(FP8X4), scales=hid_scale[:, cols],
                in_=hid_grouped[:, cols, :].rearrange("p c t -> p (c t)"),
            )
        for h, cols in enumerate(halves):
            for u, rows in enumerate(halves):
                acc = psum.tile([P, HALF], F32, name="acc%d%d" % (h, u))
                nc.tensor.matmul_mx(
                    out=acc[:], lhsT=vs_codes[:, rows].bitcast(FP4X4), lhsT_scale=vs_scale[:, rows],
                    rhs=hid_codes[:, cols].bitcast(FP8X4), rhs_scale=hid_scale[:, cols], start=True, stop=True,
                )
                if u == 0:
                    nc.vector.tensor_copy(out=results[u][:, cols], in_=acc[:])
                else:
                    nc.scalar.copy(out=results[u][:, cols], in_=acc[:])
                queue = nc.scalar if (h, u) == (1, 1) else nc.sync
                queue.dma_start(out=out[rows, cols], in_=results[u][:, cols])
